import numpy as np, ml_dtypes
CORES = [1,5,17,21,33,37,49,53]
N = 8
BF = ml_dtypes.bfloat16
def f(rng, *shape):
    return (rng.standard_normal(shape, dtype=np.float32) * np.exp2(rng.integers(-2, 3, shape[:-1] + (1,)))).astype(BF)
def wide(rng, *shape):
    v = f(rng, *shape).astype(np.float32); k = shape[:-2] + (1, shape[-1])
    return (v * np.exp2(rng.integers(-6, 7, k)) * (rng.random(k) > 0.0625)).astype(BF)
R, W, S, C = 16, 64, 4, 1
H = N * R
ROW, COL = np.arange(H)[None, :, None], np.arange(W)[None, None, :]
def stored(v):
    return np.ascontiguousarray(v.reshape(8, N, R, W).transpose(1, 0, 2, 3)).reshape(N, 8, R * W).astype(np.int32)
def whole(v):
    return np.ascontiguousarray(v.reshape(N, 8, R, W).transpose(1, 0, 2, 3)).reshape(8, H, W).astype(np.int64)
def field(rng):
    d = np.repeat(np.repeat(rng.integers(-1, 2, (2, 8, H // 8, W // 16)), 8, axis=2), 16, axis=3)
    d = np.roll(d, int(rng.integers(1, 8)), axis=2)
    return np.where(rng.random(d.shape) < 0.125, rng.integers(-1, 2, d.shape), d)
def inputs_of(rng, v):
    return {"vy": stored(v[0]), "vx": stored(v[1]), "img": f(rng, N, 128, C * R * W)}
def setup_inputs(rng):
    return inputs_of(rng, field(rng))
def setup_inputs_far(rng):
    v = np.zeros((2, 8, H, W), np.int64); o = rng.permutation(8)
    for k in range(8):
        v[0, o[k]] = 1 if k & 1 else -1; v[1, o[k]] = 1 if k & 2 else -1
        if k >= 4:
            m = rng.random((2, H, W)) < 0.015625
            v[:, o[k]] = np.where(m, rng.integers(-1, 2, (2, H, W)), v[:, o[k]])
    return inputs_of(rng, v)
def setup_inputs_ends(rng):
    v = field(rng); pm = np.array([-1, 1])
    for e in (0, H - 1): v[0, :, e, :] = rng.choice(pm, (8, W))
    for e in (0, W - 1): v[1, :, :, e] = rng.choice(pm, (8, H))
    v[0, :, 1, :] = np.where(rng.random((8, W)) < 0.75, -1, 1); v[0, :, H - 2, :] = np.where(rng.random((8, W)) < 0.75, 1, -1)
    v[1, :, :, 1] = np.where(rng.random((8, H)) < 0.75, -1, 1); v[1, :, :, W - 2] = np.where(rng.random((8, H)) < 0.75, 1, -1)
    o = rng.permutation(8); g, h = o[0], o[1]
    v[0, g, 0, :] = 2 * (np.arange(W) & 1) - 1; v[1, g, 0, :] = 1
    v[0, g, H - 1, :] = 2 * (np.arange(W) & 1) - 1; v[1, g, H - 1, :] = -1
    v[1, h, :, 0] = 2 * (np.arange(H) & 1) - 1; v[0, h, :, 0] = 1
    v[1, h, :, W - 1] = 2 * (np.arange(H) & 1) - 1; v[0, h, :, W - 1] = -1
    return inputs_of(rng, v)
def setup_inputs_sinks(rng):
    v = np.zeros((2, 8, H, W), np.int64); o = rng.permutation(8)
    v[1, o[1]] = 1 - 2 * (COL[0] & 1)
    v[0, o[2]] = 2 * (ROW[0] & 1) - 1
    for k in range(3, 8):
        r0, c0 = int(rng.integers(0, H)), int(rng.integers(0, W))
        if k == 3: r0 = R * int(rng.integers(1, N))
        if k == 4: r0 = R * int(rng.integers(1, N)) - 1
        v[0, o[k]] = np.sign(r0 - ROW[0]); v[1, o[k]] = np.sign(c0 - COL[0])
    return inputs_of(rng, v)
def setup_inputs_spread(rng):
    d = setup_inputs(rng); d["img"] = wide(rng, N, 128, C * R * W); return d
def check_inputs(d):
    bad = [k for k in ("vy", "vx") if not np.isin(np.asarray(d[k]), [-1, 0, 1]).all()]
    return bad + ([] if np.isfinite(np.asarray(d["img"]).astype(np.float32)).all() else ["finite"])
def place(a, b):
    return np.minimum(np.maximum(ROW + a, 0), H - 1), (COL + b) % W
def reference(vy, vx, img):
    a, b = whole(vy), whole(vx); g = np.arange(8)[:, None, None]
    for s in range(S):
        p, q = place(a, b)
        a, b = a + a[g, p, q], b + b[g, p, q]
    p, q = place(a, b)
    u = np.ascontiguousarray(img.reshape(N, 8, 16, C, R, W).transpose(1, 0, 4, 5, 2, 3)).reshape(8, H, W, 16, C)
    z = u[g, p, q].reshape(8, N, R, W, 16, C)
    return {"y": np.ascontiguousarray(z.transpose(1, 0, 4, 5, 2, 3)).reshape(N, 128, C * R * W)}

@@ -1,0 +1,498 @@
+from concourse.bass import DstId, RemoteDMATransfer
+from concourse.mybir import AluOpType, ActivationFunctionType
+
+W = 64
+SCRATCH = {
+    "raw": ("sbuf", [128, 128], "int32"),
+    "raw2": ("sbuf", [128, 2, 4, 16], "int32"),
+    "bi": ("sbuf", [128, 128], "int32"),
+    "bj": ("sbuf", [128, 128], "int32"),
+    "bse": ("sbuf", [128, 128], "int32"),
+    "b2i": ("sbuf", [128, 4, 16], "int32"),
+    "b2": ("sbuf", [128, 4, 16], "int32"),
+    "wl": ("sbuf", [128, 16], "bfloat16"),
+    "own": ("sbuf", [128, 128], "bfloat16"),
+    "vb": ("sbuf", [128, 4, 2, 16], "bfloat16"),
+    "dd": ("sbuf", [128, 64], "bfloat16"),
+    "da": ("sbuf", [128, 64], "bfloat16"),
+    "rb": ("sbuf", [128, 64], "bfloat16"),
+    "lp": ("sbuf", [128, 128], "bfloat16"),
+    "ln": ("sbuf", [128, 128], "bfloat16"),
+    "fo": ("sbuf", [128, 64], "uint16"),
+    "fs": ("sbuf", [128, 64], "uint16"),
+    "fp": ("sbuf", [128, 64], "uint16"),
+    "fn": ("sbuf", [128, 64], "uint16"),
+    "vi": ("sbuf", [128, 128], "bfloat16"),
+    "ua": ("sbuf", [128, 512], "bfloat16"),
+    "um": ("sbuf", [128, 1024], "bfloat16"),
+    "bb": ("sbuf", [128, 144], "bfloat16"),
+    "ev": ("sbuf", [128, 8], "float32"),
+    "e1": ("sbuf", [128, 8], "float32"),
+    "e2": ("sbuf", [128, 8], "float32"),
+    "pc": ("sbuf", [128, 8], "int32"),
+    "p8": ("sbuf", [128, 8], "int32"),
+    "tc": ("sbuf", [128, 8], "float32"),
+    "dti": ("sbuf", [128, 8], "float32"),
+    "dc": ("sbuf", [128, 8], "float32"),
+    "cp": ("sbuf", [128, 8], "float32"),
+    "cn": ("sbuf", [128, 8], "float32"),
+    "w0": ("sbuf", [128, 49 * 64], "bfloat16"),
+    "w1": ("sbuf", [128, 3072], "bfloat16"),
+    "w2": ("sbuf", [128, 3072], "bfloat16"),
+    "w3": ("sbuf", [128, 3072], "bfloat16"),
+    "im": ("sbuf", [128, 3072], "bfloat16"),
+    "ia": ("sbuf", [128, 3072], "bfloat16"),
+    "yt": ("sbuf", [128, 1024], "bfloat16"),
+    "off": ("sbuf", [128, 640], "uint16"),
+}
+for _k in range(8):
+    SCRATCH["ps%d" % _k] = ("psum", [128, 512], "float32")
+
+ZN = ["0O", "0F", "0L", "1O", "1F", "1L", "2A", "2B", "3A", "3B", "4A"]
+SEMAPHORES = ["ldy", "ldx", "ld2", "ldi", "gbi", "gvi", "gb2", "gdd", "gpc", "kb1", "kb2", "kb3", "pr1", "pr2",
+              "pr3", "pr4", "own", "vb", "um0", "um1", "um2", "um3", "ua", "us", "da", "rb", "bb0", "be", "bb", "t8",
+              "tc", "dc", "arrP", "arrN", "lstP", "lstN", "imgP", "imgN", "lsd", "lsl", "lsi", "sty", "ip", "pd0",
+              "pd1", "pd2", "pd3", "m0", "fo", "fs"]
+SEMAPHORES += ["u%s%d" % (b, h) for b in "OFL" for h in range(4)]
+SEMAPHORES += ["c%s%s" % (b, h) for b in "OFL" for h in "vs"]
+SEMAPHORES += ["%s%s" % (k, z) for z in ZN for k in ("wr", "of", "gv", "gs")]
+
+VMID = {"0O": 4, "0F": 6, "0L": 5, "1O": 4, "1F": 7, "1L": 7, "2A": 7, "2B": 7, "3A": 7, "3B": 8}
+VEND = {"0O": 7, "0L": 5, "1O": 8, "1L": 7, "2A": 3, "2B": 4, "3A": 7, "3B": 8}
+CMID = {"O": {"s": (0, 1, 2), "v": (3,)}, "F": {"s": (0, 2), "v": (1, 3)}, "L": {"s": (0, 2), "v": (1, 3)}}
+CEND = {"O": {"s": (0, 1, 2), "v": (3,)}, "L": {"s": (0, 1, 2), "v": (3,)}}
+
+
+def rank_program(g, core, T, topo):
+    rank = T.rank_of(core)
+    if rank is None:
+        return
+    OP, AF = AluOpType, ActivationFunctionType
+    n = len(T.cores)
+    prev = T.cores[rank - 1] if rank > 0 else None
+    nxt = T.cores[rank + 1] if rank < n - 1 else None
+    same_chip = lambda c: topo.chip(c) == topo.chip(core)
+    if prev is None:
+        late = "N"
+    elif nxt is None:
+        late = "P"
+    else:
+        late = "N" if same_chip(prev) else "P"
+    edge = prev is None or nxt is None
+    flip = late == "P"
+    sides = {"L": late}
+    if not edge:
+        sides["F"] = "P" if late == "N" else "N"
+    land = {"P": T.lp, "N": T.ln}
+    lst = {"P": T.fp, "N": T.fn}
+    bias = {"P": T.cp, "N": T.cn}
+    blk = {"P": 0, "O": 1, "N": 2}
+    vrows = VEND if edge else VMID
+    share = CEND if edge else CMID
+
+    def rows(a, b):
+        return (48 - b, 48 - a) if flip else (a, b)
+
+    if edge:
+        zones = [("1O", 1, 16, 29), ("1L", 1, 29, 44), ("2A", 2, 16, 24), ("2B", 2, 24, 40), ("3A", 3, 8, 24),
+                 ("3B", 3, 24, 40)]
+    else:
+        zones = [("1O", 1, 19, 29), ("1F", 1, 4, 19), ("1L", 1, 29, 44), ("2A", 2, 8, 24), ("2B", 2, 24, 40),
+                 ("3A", 3, 8, 24), ("3B", 3, 24, 40)]
+    zone = {}
+    col = 0
+    for name, s, a, b in zones:
+        a, b = rows(a, b)
+        zone[name] = (s, a, b, col)
+        col += 4 * (b - a)
+    ps = [T["ps%d" % k] for k in range(8)]
+    bank = {"0O": ps[4], "1O": ps[4], "1F": ps[5], "1L": ps[0], "2A": ps[6], "2B": ps[1], "3A": ps[2], "3B": ps[7]}
+    ubank = {"O": ps[0:4], "F": ps[4:8], "L": ps[0:4]}
+    erow = 31 if flip else 16
+    estep = 1 if flip else -1
+    win = [T.w0, T.w1, T.w2, T.w3]
+
+    def wrow(s, a, b, first=0, step=1):
+        d = 1 if s == 0 else 0
+        return win[s][:, (a + d) * W + first:(b + d) * W:step]
+
+    seen = {"g": set(), "t": set(), "v": set(), "s": set(), "y": set()}
+    queue = {"g": g, "t": g.tensor, "v": g.vector, "s": g.scalar, "y": g.sync}
+
+    def wait(q, name, val=1):
+        if name in seen[q]:
+            return
+        seen[q].add(name)
+        queue[q].wait_ge(T.sem[name], val)
+
+    g.sync.dma_start(T.raw[0:64, :], T.vy[:]).then_inc(T.sem.ldy, 16)
+    g.scalar.dma_start(T.raw[64:128, :], T.vx[:]).then_inc(T.sem.ldx, 16)
+    for h in range(2):
+        g.sync.dma_start(T.raw2[0:64, h, :, :], T.vy[h::2, :]).then_inc(T.sem.ld2, 16)
+        g.scalar.dma_start(T.raw2[64:128, h, :, :], T.vx[h::2, :]).then_inc(T.sem.ld2, 16)
+    g.sync.dma_start(T.im[:, 1024:2048], T.img[:]).then_inc(T.sem.ldi, 16)
+
+    xs = slice(64, 128)
+    g.iota(T.bi[:], [[64, 2], [1, 64]], 0, 128).then_inc(T.sem.gbi, 1)
+    g.iota(T.vi[:], [[-8, 8], [-64, 2], [0, 8]], 0, 1, allow_small_or_imprecise_dtypes=True).then_inc(T.sem.gvi, 1)
+    g.iota(T.b2i[:], [[16, 4], [1, 16]], 0, 64).then_inc(T.sem.gb2, 1)
+    g.iota(T.dd[:], [[-1, 64]], 0, 1, allow_small_or_imprecise_dtypes=True).then_inc(T.sem.gdd, 1)
+    g.iota(T.pc[:], [[0, 8]], 0, 1).then_inc(T.sem.gpc, 1)
+    if edge:
+        g.iota(T.dti[:], [[estep, 8]], estep, 0, allow_small_or_imprecise_dtypes=True).then_inc(T.sem.gpc, 1)
+    g.iota(T.ev[:], [[-16, 8]], 0, 1, allow_small_or_imprecise_dtypes=True).then_inc(T.sem.gpc, 1)
+
+    v, s_, t = g.vector, g.scalar, g.tensor
+    v.memset(T.w0[:, 0:W], 0.0).then_inc(T.sem.m0, 1)
+    v.memset(T.ia[:, 0:8 * W], 0.0).then_inc(T.sem.m0, 1)
+    wait("v", "gbi")
+    v.tensor_scalar(T.bj[0:64, :], T.bi[0:64, :], 6, 15, OP.logical_shift_right, OP.bitwise_and).then_inc(T.sem.kb1, 1)
+    v.tensor_scalar(T.bse[xs, :], T.bi[xs, :], 63, None, OP.bitwise_and).then_inc(T.sem.kb2, 1)
+    wait("v", "kb1")
+    v.tensor_scalar(T.bse[0:64, :], T.bj[0:64, :], 16, None, OP.add).then_inc(T.sem.kb2, 1)
+
+    def um(i):
+        v.tensor_scalar(T.um[:, i * 128:(i + 1) * 128], T.vi[:], float(i), None, OP.is_equal).then_inc(
+            T.sem["um%d" % i], 1)
+
+    wait("v", "gvi")
+    um(0)
+    um(1)
+    wait("s", "gvi")
+    for i in range(4):
+        s_.activation(T.ua[:, i * 128:(i + 1) * 128], T.vi[:], AF.Abs, bias=float(-4 - i)).then_inc(T.sem.ua, 1)
+    wait("s", "ua", 4)
+    for i in range(2):
+        s_.activation(T.um[:, 512 + i * 256:768 + i * 256], T.ua[:, i * 256:256 + i * 256], AF.Relu, bias=1.0,
+                      scale=-1.0).then_inc(T.sem.us, 1)
+    wait("s", "gdd")
+    s_.activation(T.da[0:64, :], T.dd[0:64, :], AF.Abs).then_inc(T.sem.da, 1)
+    s_.activation(T.da[xs, :], T.dd[xs, :], AF.Abs, bias=-64.0).then_inc(T.sem.da, 1)
+    wait("s", "da", 2)
+    s_.activation(T.rb[0:64, :], T.da[0:64, :], AF.Relu, bias=64.0, scale=-64.0).then_inc(T.sem.rb, 1)
+    s_.activation(T.rb[xs, :], T.da[xs, :], AF.Relu, bias=1.0, scale=-1.0).then_inc(T.sem.rb, 1)
+
+    wait("v", "ldx", 16)
+    v.tensor_scalar(T.wl[xs, 0:2], T.raw[xs, 0:128:64], 0.0, 64.0, OP.is_lt, OP.mult).then_inc(T.sem.pr1, 1)
+    v.tensor_scalar(T.wl[xs, 2:4], T.raw[xs, 63:128:64], 0.0, -64.0, OP.is_gt, OP.mult).then_inc(T.sem.pr1, 1)
+    wait("v", "ldy", 16)
+    wait("v", "kb2", 2)
+    v.tensor_tensor(T.own[:], T.raw[:], T.bse[:], OP.add).then_inc(T.sem.pr2, 1)
+    um(2)
+    wait("v", "pr1", 2)
+    wait("v", "pr2")
+    v.tensor_tensor(T.own[xs, 0:128:64], T.own[xs, 0:128:64], T.wl[xs, 0:2], OP.add).then_inc(T.sem.own, 1)
+    v.tensor_tensor(T.own[xs, 63:128:64], T.own[xs, 63:128:64], T.wl[xs, 2:4], OP.add).then_inc(T.sem.own, 1)
+
+    um(3)
+    wait("v", "gb2")
+    v.tensor_scalar(T.b2[0:64, :, :], T.b2i[0:64, :, :], 6, 15, OP.logical_shift_right, OP.bitwise_and).then_inc(
+        T.sem.kb3, 1)
+    v.tensor_scalar(T.b2[xs, :, :], T.b2i[xs, :, :], 63, None, OP.bitwise_and).then_inc(T.sem.kb3, 1)
+    wait("v", "ld2", 64)
+    v.tensor_scalar(T.wl[xs, 4:6], T.raw2[xs, :, 0, 0], 0.0, 64.0, OP.is_lt, OP.mult).then_inc(T.sem.pr3, 1)
+    v.tensor_scalar(T.wl[xs, 6:8], T.raw2[xs, :, 3, 15], 0.0, -64.0, OP.is_gt, OP.mult).then_inc(T.sem.pr3, 1)
+    wait("v", "kb3", 2)
+    for h in range(2):
+        v.tensor_tensor(T.vb[:, :, h, :], T.raw2[:, h, :, :], T.b2[:], OP.add).then_inc(T.sem.pr4, 1)
+    wait("v", "pr3", 2)
+    wait("v", "pr4", 2)
+    v.tensor_tensor(T.vb[xs, 0, :, 0], T.vb[xs, 0, :, 0], T.wl[xs, 4:6], OP.add).then_inc(T.sem.vb, 1)
+    v.tensor_tensor(T.vb[xs, 3, :, 15], T.vb[xs, 3, :, 15], T.wl[xs, 6:8], OP.add).then_inc(T.sem.vb, 1)
+
+    dests = [d for d in (prev, nxt) if d is not None]
+    offd = [d for d in dests if not same_chip(d)]
+    ond = [d for d in dests if same_chip(d)]
+    leave = [e for d in offd for e in topo.engines(core, d)]
+    small, bulk = {}, {}
+    for d in offd + ond:
+        es = [e for e in topo.engines(core, d) if not same_chip(d) or e not in leave][-8:]
+        small[d] = es if same_chip(d) else es[1::2]
+        bulk[d] = es if same_chip(d) else es[0::2]
+
+    def send(to, use, src, dst_of, arr_of, local):
+        trs, cnt = [], 0
+        for d in to:
+            rid, pid, _ = topo.addr(d)
+            mask = 0
+            for e in use[d]:
+                mask |= 1 << e
+            cnt += len(use[d])
+            side = "P" if d == nxt else "N"
+            trs.append(RemoteDMATransfer(dst_ids=[DstId(rid=rid, pnc=pid)], dma_engine_mask=mask,
+                                         remote_sem=T.sem[arr_of + side], srcs=[src], dsts=[dst_of(side)]))
+        g.remote_dma_fused(trs, local_sem=T.sem[local])
+        return cnt
+
+    NE = {sd: 8 if same_chip(c) else 4 for sd, c in (("P", prev), ("N", nxt)) if c is not None}
+    wait("g", "own", 2)
+    nls = send(offd + ond, small, T.own[:], lambda sd: land[sd][:], "arr", "lsd")
+    wait("g", "fs")
+    nll = send(offd + ond, small, T.fs[:], lambda sd: lst[sd][:], "lst", "lsl")
+    wait("g", "ldi", 16)
+    nli = 0
+    for to in (offd, ond):
+        if to:
+            nli += send(to, bulk, T.im[:, 1024:2048], lambda sd: T.im[:, blk[sd] * 1024:(blk[sd] + 1) * 1024], "img",
+                        "lsi")
+
+    def spread(b):
+        src = T.own if b == "O" else land[sides[b]]
+        if b != "O":
+            wait("t", "arr" + sides[b], NE[sides[b]])
+        for i in range(8):
+            wait("t", "um%d" % i if i < 4 else "us", 1 if i < 4 else 2)
+            t.matmul(ubank[b][i // 2][:, (i % 2) * 128:(i % 2 + 1) * 128], T.um[:, i * 128:(i + 1) * 128], src[:],
+                     True, True).then_inc(T.sem["u%s%d" % (b, i // 2)], 1)
+
+    def first_list():
+        wait("t", "rb", 2)
+        wait("t", "pr4", 2)
+        wait("t", "vb", 2)
+        for a in range(4):
+            for b in range(4):
+                t.matmul(bank["0O"][32 * a:32 * a + 32, b:64:4], T.vb[:, b, :, :], T.rb[:, 16 * a:16 * a + 16], True,
+                         True).then_inc(T.sem["wr0O"], 1)
+
+    def copies(b, qs="sv"):
+        base = 16 * blk["O" if b == "O" else sides[b]]
+        for q in qs:
+            if b != "O":
+                wait(q, "dc", 2)
+            for k in share[b][q]:
+                wait(q, "u%s%d" % (b, k), 2)
+                o, i = wrow(0, base + 4 * k, base + 4 * k + 4), ubank[b][k][:, 0:256]
+                if q == "v":
+                    if b == "O":
+                        op = v.tensor_copy(o, i)
+                    else:
+                        op = v.tensor_scalar(o, i, bias[sides[b]][:, 0:1], None, OP.add)
+                elif b == "O":
+                    op = s_.activation(o, i, AF.Copy)
+                else:
+                    op = s_.activation(o, i, AF.Identity, bias=bias[sides[b]][:, 0:1])
+                op.then_inc(T.sem["c%s%s" % (b, q)], 1)
+
+    def copied(q, b):
+        for e in "vs":
+            wait(q, "c%s%s" % (b, e), len(share[b][e]))
+
+    def pads(s):
+        wait("v", "dc", 2)
+        for d in range(1, min(2 ** s, 4) + 1):
+            r = erow + estep * d
+            v.tensor_scalar(wrow(s, r, r + 1), wrow(s, erow, erow + 1), T.dc[:, d - 1:d], None, OP.add).then_inc(
+                T.sem["pd%d" % s], 1)
+        if s == 3:
+            v.wait_ge(T.sem.pd3, 4)
+            a = erow + 1 if flip else erow - 4
+            v.tensor_scalar(wrow(s, a + 4 * estep, a + 4 * estep + 4), wrow(s, a, a + 4), T.dc[:, 3:4], None,
+                            OP.add).then_inc(T.sem.pd3, 1)
+
+    NPD = {0: 1, 1: 2, 2: 4, 3: 5}
+    STEPS = [(1, 1), (2, 2), (4, 4), (8, 8), (16, 1)]
+
+    def image_pads(steps):
+        wait("s", "ldi", 16)
+        for k in steps:
+            have, cnt = STEPS[k]
+            if k:
+                s_.wait_ge(T.sem.ip, k)
+            if flip:
+                f = erow + have
+                dst, src = (f, f + cnt), (f - cnt, f)
+            else:
+                f = erow - have + 1
+                dst, src = (f - cnt, f), (f, f + cnt)
+            s_.activation(T.im[:, dst[0] * W:dst[1] * W], T.im[:, src[0] * W:src[1] * W], AF.Copy).then_inc(
+                T.sem.ip, 1)
+
+    def turn(name, s, a, b, after):
+        wait("t", "bb")
+        for nm, val in after:
+            wait("t", nm, val)
+        m = 4 * (b - a)
+        for q in range(16):
+            mm = t.matmul(bank[name][:, 0:m], T.bb[:, 15 - q:143 - q], wrow(s, a, b, q, 16), q == 0, q == 15)
+        mm.then_inc(T.sem["wr" + name], 1)
+
+    def cast(dst, name, m, take, sem, cnt=1):
+        wait("v", "wr" + name, cnt)
+        v.tensor_scalar(dst, bank[name][:, 0:m], float(-take), None, OP.add).then_inc(T.sem[sem], 1)
+
+    def pick(q, out, w, li, sem):
+        if q == "v":
+            v.tensor_copy(out, w.indirect(li)).then_inc(T.sem["gv" + sem], 1)
+        else:
+            s_.activation(out, w.indirect(li), AF.Copy).then_inc(T.sem["gs" + sem], 1)
+
+    def halves(a, b, nv):
+        return {"v": (b - nv, b), "s": (a, b - nv)} if flip else {"v": (a, a + nv), "s": (a + nv, b)}
+
+    def win_rows(name):
+        s, a, b, c = zone[name]
+        return a - 2 ** s, b + 2 ** s
+
+    def lists(name, after):
+        s, a, b, c = zone[name]
+        turn(name, s, a, b, after)
+        cast(T.off[:, c:c + 4 * (b - a)], name, 4 * (b - a), W * win_rows(name)[0], "of" + name)
+
+    def part(name, x, y):
+        s, a, b, c = zone[name]
+        return T.off[:, c + 4 * (x - a):c + 4 * (y - a)]
+
+    def gather(name):
+        s, a, b, c = zone[name]
+        lo, hi = win_rows(name)
+        h = halves(a, b, vrows[name])
+        for q in "vs":
+            wait(q, "of" + name)
+            x, y = h[q]
+            if s < 3:
+                if edge:
+                    wait(q, "pd%d" % s, NPD[s])
+                pick(q, wrow(s + 1, x, y), wrow(s, lo, hi), part(name, x, y), name)
+            else:
+                sd = "P" if lo < 16 else "N"
+                wait(q, "ldi", 16)
+                if sd in NE:
+                    wait(q, "img" + sd, NE[sd])
+                else:
+                    wait(q, "ip", 5)
+                pick(q, T.ia[:, x * W:y * W], T.im[:, lo * W:hi * W], part(name, x, y), name)
+
+    def gather_own():
+        if edge:
+            a, b = rows(16, 31)
+            li, wl, wh = ("fs", 15, 32) if prev is None else ("fo", 16, 33)
+        else:
+            a, b, li, wl, wh = 17, 31, "fo", 16, 32
+        h = halves(a, b, vrows["0O"])
+        for q in "vs":
+            wait(q, li)
+            if edge:
+                wait(q, "pd0")
+            copied(q, "O")
+            x, y = h[q]
+            pick(q, wrow(1, x, y), wrow(0, wl, wh), T[li][:, 4 * (x - 16):4 * (y - 16)], "0O")
+
+    def gather_side(b):
+        sd = sides[b]
+        if sd == "P":
+            a, e, r0, wl, wh = 2, 16, 0, -1, 17
+            one, li, ol, oh = 16, "fs", 15, 18
+        else:
+            a, e, r0, wl, wh = 32, 46, 32, 31, 47
+            one, li, ol, oh = 31, "fo", 16, 33
+        nv = vrows["0" + b]
+        for q, x, y in (("v", a, a + nv), ("s", a + nv, e)):
+            copied(q, "O")
+            copied(q, b)
+            if q == "v":
+                wait(q, li)
+                pick(q, wrow(1, one, one + 1), wrow(0, ol, oh), T[li][:, 4 * (one - 16):4 * (one - 15)], "0" + b)
+            if sd == "P":
+                wait(q, "m0", 2)
+            wait(q, "lst" + sd, NE[sd])
+            pick(q, wrow(1, x, y), wrow(0, wl, wh), lst[sd][:, 4 * (x - r0):4 * (y - r0)], "0" + b)
+
+    def shifts():
+        wait("v", "t8")
+        if edge:
+            v.tensor_scalar(T.tc[:], T.p8[:], 0.0, None, OP.is_equal).then_inc(T.sem.tc, 1)
+        for sd, val in (("P", -16.0), ("N", 16.0)):
+            if sd in sides.values():
+                v.tensor_scalar(bias[sd][:], T.p8[:], 0.0, val, OP.is_equal, OP.mult).then_inc(T.sem.dc, 1)
+        if edge:
+            wait("v", "tc")
+            v.tensor_tensor(T.dc[:], T.dti[:], T.tc[:], OP.mult).then_inc(T.sem.dc, 1)
+
+    def list_maker():
+        v.memset(T.bb[:], 0.0).then_inc(T.sem.bb0, 1)
+        v.tensor_scalar(T.e1[:], T.ev[:], 0.0, 64.0, OP.is_equal, OP.mult).then_inc(T.sem.be, 1)
+        v.tensor_scalar(T.e2[:], T.ev[:], 8.0, None, OP.is_equal).then_inc(T.sem.be, 1)
+        wait("v", "be", 2)
+        wait("v", "bb0")
+        v.tensor_tensor(T.bb[:, 15:143:16], T.e1[:], T.e2[:], OP.add).then_inc(T.sem.bb, 1)
+
+    def both(name, nv=1):
+        return [("gv" + name, nv), ("gs" + name, 1)]
+
+    wait("t", "own", 2)
+    spread("O")
+    first_list()
+    copies("O")
+    wait("v", "gpc", 3 if edge else 2)
+    v.tensor_scalar(T.p8[:], T.pc[:], 8, None, OP.bitwise_and).then_inc(T.sem.t8, 1)
+    cast(T.fs[:], "0O", 64, -W, "fs", 16)
+    cast(T.fo[:], "0O", 64, 0, "fo", 16)
+    wait("t", "fs")
+    wait("t", "fo")
+    copied("t", "O")
+    if edge:
+        shifts()
+        copied("v", "O")
+        pads(0)
+        image_pads((0, 1, 2))
+        gather_own()
+        list_maker()
+        spread("L")
+        wait("v", "gv0O")
+        pads(1)
+        copies("L")
+        gather_side("L")
+        lists("1O", both("0O"))
+        gather("1O")
+        image_pads((3, 4))
+        lists("1L", both("0O") + both("0L", 2))
+        wait("v", "gv1O")
+        pads(2)
+        gather("1L")
+        lists("2A", both("1O"))
+        gather("2A")
+        lists("2B", both("1O") + both("1L"))
+        wait("v", "gv2A")
+        pads(3)
+        gather("2B")
+        lists("3A", both("2A") + [("pd3", NPD[3])])
+    else:
+        shifts()
+        gather_own()
+        list_maker()
+        spread("F")
+        spread("L")
+        copies("F")
+        gather_side("F")
+        copies("L")
+        gather_side("L")
+        lists("1O", both("0O") + [("cFv", 2), ("cFs", 2)])
+        gather("1O")
+        lists("1F", both("0O") + both("0F", 2))
+        gather("1F")
+        lists("1L", both("0O") + both("0L", 2))
+        gather("1L")
+        lists("2A", both("1O") + both("1F"))
+        gather("2A")
+        lists("2B", both("1O") + both("1L"))
+        gather("2B")
+        lists("3A", both("2A"))
+    gather("3A")
+    lists("3B", both("2B"))
+    gather("3B")
+    h = halves(16, 32, 8)
+    for q in "vs":
+        for nm, val in both("3A") + both("3B"):
+            wait(q, nm, val)
+        wait(q, "m0", 2)
+        x, y = h[q]
+        z = [k for k in ("3A", "3B") if zone[k][1] <= x and y <= zone[k][2]][0]
+        lo, hi = win_rows(z)
+        pick(q, T.yt[:, (x - 16) * W:(y - 16) * W], T.ia[:, lo * W:min(hi, 40) * W], part(z, x, y), "4A")
+    wait("y", "gv4A")
+    wait("y", "gs4A")
+    g.sync.dma_start(T.y[:], T.yt[:]).then_inc(T.sem.sty, 16)
+    wait("y", "sty", 16)
+    wait("g", "lsd", nls)
+    wait("g", "lsl", nll)
+    wait("g", "lsi", nli)

@@ -7,7 +7,6 @@ SCRATCH = {
     "raw2": ("sbuf", [128, 2, 4, 16], "int32"),
     "bi": ("sbuf", [128, 128], "int32"),
     "bj": ("sbuf", [128, 128], "int32"),
-    "bse": ("sbuf", [128, 128], "int32"),
     "b2i": ("sbuf", [128, 4, 16], "int32"),
     "b2": ("sbuf", [128, 4, 16], "int32"),
     "wl": ("sbuf", [128, 16], "bfloat16"),
@@ -48,19 +47,21 @@ SCRATCH = {
 for _k in range(8):
     SCRATCH["ps%d" % _k] = ("psum", [128, 512], "float32")
 
-ZN = ["0O", "0F", "0L", "1O", "1F", "1L", "2A", "2B", "3A", "3B", "4A"]
+ZN = ["0O", "0F", "0L", "1O", "1F", "1L", "2O", "2F", "2L", "3F", "3L", "4F", "4L"]
 SEMAPHORES = ["ldy", "ldx", "ld2", "ldi", "gbi", "gvi", "gb2", "gdd", "gpc", "kb1", "kb2", "kb3", "pr1", "pr2",
               "pr3", "pr4", "own", "vb", "um0", "um1", "um2", "um3", "ua", "us", "da", "rb", "bb0", "be", "bb", "t8",
-              "tc", "dc", "arrP", "arrN", "lstP", "lstN", "imgP", "imgN", "lsd", "lsl", "lsi", "sty", "ip", "pd0",
-              "pd1", "pd2", "pd3", "m0", "fo", "fs"]
+              "tc", "dc", "arrP", "arrN", "lstP", "lstN", "imgP", "imgN", "iarP", "iarN", "lsd", "lsl", "lsi", "lsa",
+              "sty", "ip", "pd0", "pd1", "pd2", "pd3", "m0", "fo", "fs"]
 SEMAPHORES += ["u%s%d" % (b, h) for b in "OFL" for h in range(4)]
 SEMAPHORES += ["c%s%s" % (b, h) for b in "OFL" for h in "vs"]
 SEMAPHORES += ["%s%s" % (k, z) for z in ZN for k in ("wr", "of", "gv", "gs")]
 
-VMID = {"0O": 4, "0F": 6, "0L": 5, "1O": 4, "1F": 7, "1L": 7, "2A": 7, "2B": 7, "3A": 7, "3B": 8}
-VEND = {"0O": 7, "0L": 5, "1O": 8, "1L": 7, "2A": 3, "2B": 4, "3A": 7, "3B": 8}
-CMID = {"O": {"s": (0, 1, 2), "v": (3,)}, "F": {"s": (0, 2), "v": (1, 3)}, "L": {"s": (0, 2), "v": (1, 3)}}
-CEND = {"O": {"s": (0, 1, 2), "v": (3,)}, "L": {"s": (0, 1, 2), "v": (3,)}}
+ZONES = {"1F": (7, [("1F", 12, 28, 7)]), "1L": (4, [("1L", 28, 44, 7)]), "2F": (5, [("2F", 16, 28, 5)]),
+         "2L": (0, [("2L", 28, 40, 6)]), "3F": (6, [("3F", 16, 24, 4)]), "3L": (1, [("3L", 24, 40, 8)])}
+ZEND = {"1O": (7, [("1O", 19, 32, 6)]), "1F": (0, [("1F", 12, 19, 3)]), "2O": (1, [("2L", 24, 32, 4)]),
+        "2F": (2, [("2F", 16, 24, 4)]), "3F": (4, [("3F", 16, 24, 4)]), "3L": (3, [("3L", 24, 40, 8)])}
+ORDER = "uF uL cF 0F cL 0L t1F 1F t1L 1L t2F 2F t2L 2L t3F 3F t3L 3L 4L 4F".split()
+OEND = "uF t1O p1 cF 0F t1F 1O 1F t2F t2O p2 ia 2F 2L t3F p3 ib t3L 3F 3L 4L 4F".split()
 
 
 def rank_program(g, core, T, topo):
@@ -71,45 +72,38 @@ def rank_program(g, core, T, topo):
     n = len(T.cores)
     prev = T.cores[rank - 1] if rank > 0 else None
     nxt = T.cores[rank + 1] if rank < n - 1 else None
-    same_chip = lambda c: topo.chip(c) == topo.chip(core)
-    if prev is None:
-        late = "N"
-    elif nxt is None:
-        late = "P"
-    else:
-        late = "N" if same_chip(prev) else "P"
+    same_chip = lambda c: c is not None and topo.chip(c) == topo.chip(core)
+    flip = same_chip(nxt)
     edge = prev is None or nxt is None
-    flip = late == "P"
-    sides = {"L": late}
+    sides = {"F": "N" if flip else "P"}
     if not edge:
-        sides["F"] = "P" if late == "N" else "N"
+        sides["L"] = "P" if flip else "N"
     land = {"P": T.lp, "N": T.ln}
     lst = {"P": T.fp, "N": T.fn}
     bias = {"P": T.cp, "N": T.cn}
     blk = {"P": 0, "O": 1, "N": 2}
-    vrows = VEND if edge else VMID
-    share = CEND if edge else CMID
+    vrows = {"0O": 6 if edge else 4, "0F": 2, "0L": 6}
+    share = {"O": {"s": (0, 1, 2), "v": (3,)}, "F": {"s": (0,), "v": (1,)} if flip else {"s": (2,), "v": (3,)},
+             "L": {"s": (0, 2), "v": (1, 3)}}
 
     def rows(a, b):
         return (48 - b, 48 - a) if flip else (a, b)
 
-    if edge:
-        zones = [("1O", 1, 16, 29), ("1L", 1, 29, 44), ("2A", 2, 16, 24), ("2B", 2, 24, 40), ("3A", 3, 8, 24),
-                 ("3B", 3, 24, 40)]
-    else:
-        zones = [("1O", 1, 19, 29), ("1F", 1, 4, 19), ("1L", 1, 29, 44), ("2A", 2, 8, 24), ("2B", 2, 24, 40),
-                 ("3A", 3, 8, 24), ("3B", 3, 24, 40)]
-    zone = {}
+    zone, piece = {}, {}
     col = 0
-    for name, s, a, b in zones:
-        a, b = rows(a, b)
-        zone[name] = (s, a, b, col)
-        col += 4 * (b - a)
+    for name, (bk, parts) in (ZEND if edge else ZONES).items():
+        zone[name] = (int(name[0]),) + rows(parts[0][1], parts[-1][2]) + (bk,)
+        for pn, a, b, nv in parts:
+            piece[pn] = (name,) + rows(a, b) + (nv, col)
+            col += 4 * (b - a)
     ps = [T["ps%d" % k] for k in range(8)]
-    bank = {"0O": ps[4], "1O": ps[4], "1F": ps[5], "1L": ps[0], "2A": ps[6], "2B": ps[1], "3A": ps[2], "3B": ps[7]}
-    ubank = {"O": ps[0:4], "F": ps[4:8], "L": ps[0:4]}
-    erow = 31 if flip else 16
-    estep = 1 if flip else -1
+    bank = {z: ps[zone[z][3]] for z in zone}
+    bank["0O"] = ps[4]
+    ubank = {"O": ps[0:4], "F": [ps[5], ps[6], ps[5], ps[6]], "L": ps[0:4]}
+    bse = ps[7]
+    erow = 16 if flip else 31
+    estep = -1 if flip else 1
+    up = estep > 0
     win = [T.w0, T.w1, T.w2, T.w3]
 
     def wrow(s, a, b, first=0, step=1):
@@ -143,13 +137,17 @@ def rank_program(g, core, T, topo):
     g.iota(T.ev[:], [[-16, 8]], 0, 1, allow_small_or_imprecise_dtypes=True).then_inc(T.sem.gpc, 1)
 
     v, s_, t = g.vector, g.scalar, g.tensor
-    v.memset(T.w0[:, 0:W], 0.0).then_inc(T.sem.m0, 1)
-    v.memset(T.ia[:, 0:8 * W], 0.0).then_inc(T.sem.m0, 1)
+    if flip:
+        v.memset(T.w0[:, 0:W], 0.0).then_inc(T.sem.m0, 1)
+        v.memset(T.ia[:, 0:8 * W], 0.0).then_inc(T.sem.m0, 1)
+    else:
+        v.memset(T.w0[:, 0:9 * W], 0.0).then_inc(T.sem.m0, 2)
     wait("v", "gbi")
     v.tensor_scalar(T.bj[0:64, :], T.bi[0:64, :], 6, 15, OP.logical_shift_right, OP.bitwise_and).then_inc(T.sem.kb1, 1)
-    v.tensor_scalar(T.bse[xs, :], T.bi[xs, :], 63, None, OP.bitwise_and).then_inc(T.sem.kb2, 1)
-    wait("v", "kb1")
-    v.tensor_scalar(T.bse[0:64, :], T.bj[0:64, :], 16, None, OP.add).then_inc(T.sem.kb2, 1)
+    v.tensor_scalar(T.bj[xs, :], T.bi[xs, :], 63, None, OP.bitwise_and).then_inc(T.sem.kb1, 1)
+    wait("v", "kb1", 2)
+    v.tensor_scalar(bse[0:64, 0:128], T.bj[0:64, :], 16.0, None, OP.add).then_inc(T.sem.kb2, 1)
+    v.tensor_scalar(bse[xs, 0:128], T.bj[xs, :], 0.0, None, OP.add).then_inc(T.sem.kb2, 1)
 
     def um(i):
         v.tensor_scalar(T.um[:, i * 128:(i + 1) * 128], T.vi[:], float(i), None, OP.is_equal).then_inc(
@@ -173,11 +171,11 @@ def rank_program(g, core, T, topo):
     s_.activation(T.rb[xs, :], T.da[xs, :], AF.Relu, bias=1.0, scale=-1.0).then_inc(T.sem.rb, 1)
 
     wait("v", "ldx", 16)
-    v.tensor_scalar(T.wl[xs, 0:2], T.raw[xs, 0:128:64], 0.0, 64.0, OP.is_lt, OP.mult).then_inc(T.sem.pr1, 1)
-    v.tensor_scalar(T.wl[xs, 2:4], T.raw[xs, 63:128:64], 0.0, -64.0, OP.is_gt, OP.mult).then_inc(T.sem.pr1, 1)
     wait("v", "ldy", 16)
     wait("v", "kb2", 2)
-    v.tensor_tensor(T.own[:], T.raw[:], T.bse[:], OP.add).then_inc(T.sem.pr2, 1)
+    v.tensor_tensor(T.own[:], T.raw[:], bse[:, 0:128], OP.add).then_inc(T.sem.pr2, 1)
+    v.tensor_scalar(T.wl[xs, 0:2], T.raw[xs, 0:128:64], 0.0, 64.0, OP.is_lt, OP.mult).then_inc(T.sem.pr1, 1)
+    v.tensor_scalar(T.wl[xs, 2:4], T.raw[xs, 63:128:64], 0.0, -64.0, OP.is_gt, OP.mult).then_inc(T.sem.pr1, 1)
     um(2)
     wait("v", "pr1", 2)
     wait("v", "pr2")
@@ -204,11 +202,8 @@ def rank_program(g, core, T, topo):
     offd = [d for d in dests if not same_chip(d)]
     ond = [d for d in dests if same_chip(d)]
     leave = [e for d in offd for e in topo.engines(core, d)]
-    small, bulk = {}, {}
-    for d in offd + ond:
-        es = [e for e in topo.engines(core, d) if not same_chip(d) or e not in leave][-8:]
-        small[d] = es if same_chip(d) else es[1::2]
-        bulk[d] = es if same_chip(d) else es[0::2]
+    half = {d: [e for e in topo.engines(core, d) if not same_chip(d) or e not in leave][-8:] for d in dests}
+    every = {d: topo.engines(core, d) for d in ond}
 
     def send(to, use, src, dst_of, arr_of, local):
         trs, cnt = [], 0
@@ -224,23 +219,33 @@ def rank_program(g, core, T, topo):
         g.remote_dma_fused(trs, local_sem=T.sem[local])
         return cnt
 
-    NE = {sd: 8 if same_chip(c) else 4 for sd, c in (("P", prev), ("N", nxt)) if c is not None}
+    NE = {sd: len(half[c]) for sd, c in (("P", prev), ("N", nxt)) if c is not None}
+    NA = len(topo.engines(ond[0], core))
+    near = rows(16, 24)
+    there = {"P": (8, 16), "N": (32, 40)}
     wait("g", "own", 2)
-    nls = send(offd + ond, small, T.own[:], lambda sd: land[sd][:], "arr", "lsd")
+    nls = send(offd + ond, half, T.own[:], lambda sd: land[sd][:], "arr", "lsd")
     wait("g", "fs")
-    nll = send(offd + ond, small, T.fs[:], lambda sd: lst[sd][:], "lst", "lsl")
+    nll = send(offd + ond, half, T.fs[:], lambda sd: lst[sd][:], "lst", "lsl")
     wait("g", "ldi", 16)
     nli = 0
-    for to in (offd, ond):
-        if to:
-            nli += send(to, bulk, T.im[:, 1024:2048], lambda sd: T.im[:, blk[sd] * 1024:(blk[sd] + 1) * 1024], "img",
-                        "lsi")
+    if offd:
+        nli += send(offd, half, T.im[:, 1024:2048], lambda sd: T.im[:, blk[sd] * 1024:(blk[sd] + 1) * 1024], "img",
+                    "lsi")
+    nli += send(ond, half, T.im[:, near[0] * W:near[1] * W], lambda sd: T.im[:, there[sd][0] * W:there[sd][1] * W],
+                "img", "lsi")
+    wait("g", "gv3F")
+    wait("g", "gs3F")
+    nla = send(ond, every, T.ia[:, near[0] * W:near[1] * W], lambda sd: T.ia[:, there[sd][0] * W:there[sd][1] * W],
+               "iar", "lsa")
 
     def spread(b):
         src = T.own if b == "O" else land[sides[b]]
         if b != "O":
             wait("t", "arr" + sides[b], NE[sides[b]])
         for i in range(8):
+            if i // 2 not in share[b]["s"] + share[b]["v"]:
+                continue
             wait("t", "um%d" % i if i < 4 else "us", 1 if i < 4 else 2)
             t.matmul(ubank[b][i // 2][:, (i % 2) * 128:(i % 2 + 1) * 128], T.um[:, i * 128:(i + 1) * 128], src[:],
                      True, True).then_inc(T.sem["u%s%d" % (b, i // 2)], 1)
@@ -285,7 +290,7 @@ def rank_program(g, core, T, topo):
                 T.sem["pd%d" % s], 1)
         if s == 3:
             v.wait_ge(T.sem.pd3, 4)
-            a = erow + 1 if flip else erow - 4
+            a = erow + 1 if up else erow - 4
             v.tensor_scalar(wrow(s, a + 4 * estep, a + 4 * estep + 4), wrow(s, a, a + 4), T.dc[:, 3:4], None,
                             OP.add).then_inc(T.sem.pd3, 1)
 
@@ -298,7 +303,7 @@ def rank_program(g, core, T, topo):
             have, cnt = STEPS[k]
             if k:
                 s_.wait_ge(T.sem.ip, k)
-            if flip:
+            if up:
                 f = erow + have
                 dst, src = (f, f + cnt), (f - cnt, f)
             else:
@@ -306,15 +311,6 @@ def rank_program(g, core, T, topo):
                 dst, src = (f - cnt, f), (f, f + cnt)
             s_.activation(T.im[:, dst[0] * W:dst[1] * W], T.im[:, src[0] * W:src[1] * W], AF.Copy).then_inc(
                 T.sem.ip, 1)
-
-    def turn(name, s, a, b, after):
-        wait("t", "bb")
-        for nm, val in after:
-            wait("t", nm, val)
-        m = 4 * (b - a)
-        for q in range(16):
-            mm = t.matmul(bank[name][:, 0:m], T.bb[:, 15 - q:143 - q], wrow(s, a, b, q, 16), q == 0, q == 15)
-        mm.then_inc(T.sem["wr" + name], 1)
 
     def cast(dst, name, m, take, sem, cnt=1):
         wait("v", "wr" + name, cnt)
@@ -329,42 +325,64 @@ def rank_program(g, core, T, topo):
     def halves(a, b, nv):
         return {"v": (b - nv, b), "s": (a, b - nv)} if flip else {"v": (a, a + nv), "s": (a + nv, b)}
 
-    def win_rows(name):
-        s, a, b, c = zone[name]
-        return a - 2 ** s, b + 2 ** s
+    def both(name, nv=1):
+        return [("gv" + name, nv), ("gs" + name, 1)]
 
-    def lists(name, after):
-        s, a, b, c = zone[name]
-        turn(name, s, a, b, after)
-        cast(T.off[:, c:c + 4 * (b - a)], name, 4 * (b - a), W * win_rows(name)[0], "of" + name)
+    made = {1: [(rows(17, 32 if edge else 31), both("0O")), (rows(10, 17), both("0F", 2))], 2: [], 3: [], 4: []}
+    if edge:
+        for s in (1, 2, 3):
+            made[s].append((rows(32, 32 + 2 ** s), [("pd%d" % s, NPD[s])]))
+    else:
+        made[1].append((rows(31, 46), both("0L", 2)))
+    for pn, (z, a, b, nv, c) in piece.items():
+        made[zone[z][0] + 1].append(((a, b), both(pn)))
+    made[4].append((rows(8, 16), [("iar" + sides["F"], NA)]))
 
-    def part(name, x, y):
-        s, a, b, c = zone[name]
+    def ready(q, s, a, b):
+        for (x, y), sems in made[s]:
+            if x < b and a < y:
+                for nm, val in sems:
+                    wait(q, nm, val)
+
+    def turn(name):
+        s, a, b, bk = zone[name]
+        ready("t", s, a, b)
+        wait("t", "bb")
+        m = 4 * (b - a)
+        for q in range(16):
+            mm = t.matmul(bank[name][:, 0:m], T.bb[:, 15 - q:143 - q], wrow(s, a, b, q, 16), q == 0, q == 15)
+        mm.then_inc(T.sem["wr" + name], 1)
+
+    def part(pn, x, y):
+        z, a, b, nv, c = piece[pn]
         return T.off[:, c + 4 * (x - a):c + 4 * (y - a)]
 
-    def gather(name):
-        s, a, b, c = zone[name]
-        lo, hi = win_rows(name)
-        h = halves(a, b, vrows[name])
+    def gather(pn):
+        z, a, b, nv, c = piece[pn]
+        s, za = zone[z][0:2]
+        lo, hi = a - 2 ** s, b + 2 ** s
+        wait("v", "wr" + z)
+        v.tensor_scalar(part(pn, a, b), bank[z][:, 4 * (a - za):4 * (b - za)], float(-W * lo), None, OP.add).then_inc(
+            T.sem["of" + pn], 1)
+        h = halves(a, b, nv)
         for q in "vs":
-            wait(q, "of" + name)
+            wait(q, "of" + pn)
             x, y = h[q]
             if s < 3:
-                if edge:
-                    wait(q, "pd%d" % s, NPD[s])
-                pick(q, wrow(s + 1, x, y), wrow(s, lo, hi), part(name, x, y), name)
+                ready(q, s, lo, hi)
+                pick(q, wrow(s + 1, x, y), wrow(s, lo, hi), part(pn, x, y), pn)
             else:
-                sd = "P" if lo < 16 else "N"
                 wait(q, "ldi", 16)
-                if sd in NE:
-                    wait(q, "img" + sd, NE[sd])
-                else:
-                    wait(q, "ip", 5)
-                pick(q, T.ia[:, x * W:y * W], T.im[:, lo * W:hi * W], part(name, x, y), name)
+                for sd, out in (("P", lo < 16), ("N", hi > 32)):
+                    if out and sd in NE:
+                        wait(q, "img" + sd, NE[sd])
+                    elif out:
+                        wait(q, "ip", 5)
+                pick(q, T.ia[:, x * W:y * W], T.im[:, lo * W:hi * W], part(pn, x, y), pn)
 
     def gather_own():
         if edge:
-            a, b = rows(16, 31)
+            a, b = rows(17, 32)
             li, wl, wh = ("fs", 15, 32) if prev is None else ("fo", 16, 33)
         else:
             a, b, li, wl, wh = 17, 31, "fo", 16, 32
@@ -379,11 +397,12 @@ def rank_program(g, core, T, topo):
 
     def gather_side(b):
         sd = sides[b]
+        cnt = 6 if b == "F" else 14
         if sd == "P":
-            a, e, r0, wl, wh = 2, 16, 0, -1, 17
+            a, e, r0, wl, wh = 16 - cnt, 16, 0, -1, 17
             one, li, ol, oh = 16, "fs", 15, 18
         else:
-            a, e, r0, wl, wh = 32, 46, 32, 31, 47
+            a, e, r0, wl, wh = 32, 32 + cnt, 32, 31, 33 + cnt
             one, li, ol, oh = 31, "fo", 16, 33
         nv = vrows["0" + b]
         for q, x, y in (("v", a, a + nv), ("s", a + nv, e)):
@@ -396,6 +415,21 @@ def rank_program(g, core, T, topo):
                 wait(q, "m0", 2)
             wait(q, "lst" + sd, NE[sd])
             pick(q, wrow(1, x, y), wrow(0, wl, wh), lst[sd][:, 4 * (x - r0):4 * (y - r0)], "0" + b)
+
+    def last(b):
+        a, e = rows(16, 24) if b == "F" else rows(24, 32)
+        h = halves(a, e, 4)
+        for q in "vs":
+            x, y = h[q]
+            pn = [k for k in piece if k[0] == "3" and piece[k][1] <= x and y <= piece[k][2]][0]
+            lo = piece[pn][1] - 8
+            ready(q, 4, lo, y + 8)
+            wait(q, "m0", 2)
+            pick(q, T.yt[:, (x - 16) * W:(y - 16) * W], T.ia[:, lo * W:(y + 8) * W], part(pn, x, y), "4" + b)
+        for nm, val in both("4" + b):
+            wait("y", nm, val)
+        cols = slice((a - 16) * W, (e - 16) * W)
+        g.sync.dma_start(T.y[:, cols], T.yt[:, cols]).then_inc(T.sem.sty, 16)
 
     def shifts():
         wait("v", "t8")
@@ -416,9 +450,6 @@ def rank_program(g, core, T, topo):
         wait("v", "bb0")
         v.tensor_tensor(T.bb[:, 15:143:16], T.e1[:], T.e2[:], OP.add).then_inc(T.sem.bb, 1)
 
-    def both(name, nv=1):
-        return [("gv" + name, nv), ("gs" + name, 1)]
-
     wait("t", "own", 2)
     spread("O")
     first_list()
@@ -427,72 +458,36 @@ def rank_program(g, core, T, topo):
     v.tensor_scalar(T.p8[:], T.pc[:], 8, None, OP.bitwise_and).then_inc(T.sem.t8, 1)
     cast(T.fs[:], "0O", 64, -W, "fs", 16)
     cast(T.fo[:], "0O", 64, 0, "fo", 16)
+    shifts()
+    if edge:
+        copied("v", "O")
+        pads(0)
+    gather_own()
+    list_maker()
     wait("t", "fs")
     wait("t", "fo")
     copied("t", "O")
-    if edge:
-        shifts()
-        copied("v", "O")
-        pads(0)
-        image_pads((0, 1, 2))
-        gather_own()
-        list_maker()
-        spread("L")
-        wait("v", "gv0O")
-        pads(1)
-        copies("L")
-        gather_side("L")
-        lists("1O", both("0O"))
-        gather("1O")
-        image_pads((3, 4))
-        lists("1L", both("0O") + both("0L", 2))
-        wait("v", "gv1O")
-        pads(2)
-        gather("1L")
-        lists("2A", both("1O"))
-        gather("2A")
-        lists("2B", both("1O") + both("1L"))
-        wait("v", "gv2A")
-        pads(3)
-        gather("2B")
-        lists("3A", both("2A") + [("pd3", NPD[3])])
-    else:
-        shifts()
-        gather_own()
-        list_maker()
-        spread("F")
-        spread("L")
-        copies("F")
-        gather_side("F")
-        copies("L")
-        gather_side("L")
-        lists("1O", both("0O") + [("cFv", 2), ("cFs", 2)])
-        gather("1O")
-        lists("1F", both("0O") + both("0F", 2))
-        gather("1F")
-        lists("1L", both("0O") + both("0L", 2))
-        gather("1L")
-        lists("2A", both("1O") + both("1F"))
-        gather("2A")
-        lists("2B", both("1O") + both("1L"))
-        gather("2B")
-        lists("3A", both("2A"))
-    gather("3A")
-    lists("3B", both("2B"))
-    gather("3B")
-    h = halves(16, 32, 8)
-    for q in "vs":
-        for nm, val in both("3A") + both("3B"):
-            wait(q, nm, val)
-        wait(q, "m0", 2)
-        x, y = h[q]
-        z = [k for k in ("3A", "3B") if zone[k][1] <= x and y <= zone[k][2]][0]
-        lo, hi = win_rows(z)
-        pick(q, T.yt[:, (x - 16) * W:(y - 16) * W], T.ia[:, lo * W:min(hi, 40) * W], part(z, x, y), "4A")
-    wait("y", "gv4A")
-    wait("y", "gs4A")
-    g.sync.dma_start(T.y[:], T.yt[:]).then_inc(T.sem.sty, 16)
-    wait("y", "sty", 16)
+    for step in (OEND if edge else ORDER):
+        k, b = step[0], step[1:]
+        if k == "u":
+            spread(b)
+        elif k == "c":
+            copies(b)
+        elif k == "0":
+            gather_side(b)
+        elif k == "4":
+            last(b)
+        elif k == "t":
+            turn(b)
+        elif k == "p":
+            ready("v", int(b), erow, erow + 1)
+            pads(int(b))
+        elif k == "i":
+            image_pads((0, 1, 2) if b == "a" else (3, 4))
+        else:
+            gather(step)
+    wait("y", "sty", 32)
     wait("g", "lsd", nls)
     wait("g", "lsl", nll)
     wait("g", "lsi", nli)
+    wait("g", "lsa", nla)

@@ -47,7 +47,7 @@ SCRATCH = {
 for _k in range(8):
     SCRATCH["ps%d" % _k] = ("psum", [128, 512], "float32")
 
-ZN = ["0O", "0F", "0L", "1O", "1F", "1L", "2O", "2F", "2L", "3F", "3L", "4F", "4L"]
+ZN = ["0O", "0F", "0L", "1O", "1F", "1L", "1X", "1Y", "2O", "2F", "2L", "3F", "3M", "3L", "4F", "4L"]
 SEMAPHORES = ["ldy", "ldx", "ld2", "ldi", "gbi", "gvi", "gb2", "gdd", "gpc", "kb1", "kb2", "kb3", "pr1", "pr2",
               "pr3", "pr4", "own", "vb", "um0", "um1", "um2", "um3", "ua", "us", "da", "rb", "bb0", "be", "bb", "t8",
               "tc", "dc", "arrP", "arrN", "lstP", "lstN", "imgP", "imgN", "iarP", "iarN", "lsd", "lsl", "lsi", "lsa",
@@ -56,12 +56,16 @@ SEMAPHORES += ["u%s%d" % (b, h) for b in "OFL" for h in range(4)]
 SEMAPHORES += ["c%s%s" % (b, h) for b in "OFL" for h in "vs"]
 SEMAPHORES += ["%s%s" % (k, z) for z in ZN for k in ("wr", "of", "gv", "gs")]
 
-ZONES = {"1F": (7, [("1F", 12, 28, 7)]), "1L": (4, [("1L", 28, 44, 7)]), "2F": (5, [("2F", 16, 28, 5)]),
-         "2L": (0, [("2L", 28, 40, 6)]), "3F": (6, [("3F", 16, 24, 4)]), "3L": (1, [("3L", 24, 40, 8)])}
+ZONES = {"1O": (7, [("1O", 19, 29, 4)]), "1F": (4, [("1X", 12, 16, 2), ("1F", 16, 19, 2)]),
+         "1L": (0, [("1L", 29, 40, 5), ("1Y", 40, 44, 2)]), "2F": (5, [("2F", 16, 24, 4), ("2O", 24, 29, 2)]),
+         "2L": (1, [("2L", 29, 40, 5)]), "3F": (6, [("3F", 16, 24, 4)]), "3M": (3, [("3M", 24, 28, 1)]),
+         "3L": (2, [("3L", 28, 40, 6)])}
 ZEND = {"1O": (7, [("1O", 19, 32, 6)]), "1F": (0, [("1F", 12, 19, 3)]), "2O": (1, [("2L", 24, 32, 4)]),
         "2F": (2, [("2F", 16, 24, 4)]), "3F": (4, [("3F", 16, 24, 4)]), "3L": (3, [("3L", 24, 40, 8)])}
-ORDER = "uF uL cF 0F cL 0L t1F 1F t1L 1L t2F 2F t2L 2L t3F 3F t3L 3L 4L 4F".split()
-OEND = "uF t1O p1 cF 0F t1F 1O 1F t2F t2O p2 ia 2F 2L t3F p3 ib t3L 3F 3L 4L 4F".split()
+ORDER = ("uF uL t1O cF cL 0F k1O t1F 0L g1O t1L k1F k1X g1F t2F k1L g1X k1Y g1L t2L k2F k2O g2F t3F g1Y k2L g2O "
+         "t3M g2L t3L g3F k3M k3L g3M g3L 4L 4F").split()
+OEND = ("uF t1O i0 cF p1 i1 0F t1F k1O g1O t2O k1F i2 g1F t2F p2 k2L g2L k2F g2F t3F i3 p3 i4 t3L g3F g3L "
+        "4L 4F").split()
 
 
 def rank_program(g, core, T, topo):
@@ -82,7 +86,7 @@ def rank_program(g, core, T, topo):
     lst = {"P": T.fp, "N": T.fn}
     bias = {"P": T.cp, "N": T.cn}
     blk = {"P": 0, "O": 1, "N": 2}
-    vrows = {"0O": 6 if edge else 4, "0F": 2, "0L": 6}
+    vrows = {"0O": 6, "0F": 2, "0L": 6}
     share = {"O": {"s": (0, 1, 2), "v": (3,)}, "F": {"s": (0,), "v": (1,)} if flip else {"s": (2,), "v": (3,)},
              "L": {"s": (0, 2), "v": (1, 3)}}
 
@@ -159,16 +163,21 @@ def rank_program(g, core, T, topo):
     wait("s", "gvi")
     for i in range(4):
         s_.activation(T.ua[:, i * 128:(i + 1) * 128], T.vi[:], AF.Abs, bias=float(-4 - i)).then_inc(T.sem.ua, 1)
+    wait("s", "gdd")
+    s_.activation(T.da[0:64, :], T.dd[0:64, :], AF.Abs).then_inc(T.sem.da, 1)
+    s_.activation(T.da[xs, :], T.dd[xs, :], AF.Abs, bias=-64.0).then_inc(T.sem.da, 1)
     wait("s", "ua", 4)
     for i in range(2):
         s_.activation(T.um[:, 512 + i * 256:768 + i * 256], T.ua[:, i * 256:256 + i * 256], AF.Relu, bias=1.0,
                       scale=-1.0).then_inc(T.sem.us, 1)
-    wait("s", "gdd")
-    s_.activation(T.da[0:64, :], T.dd[0:64, :], AF.Abs).then_inc(T.sem.da, 1)
-    s_.activation(T.da[xs, :], T.dd[xs, :], AF.Abs, bias=-64.0).then_inc(T.sem.da, 1)
     wait("s", "da", 2)
     s_.activation(T.rb[0:64, :], T.da[0:64, :], AF.Relu, bias=64.0, scale=-64.0).then_inc(T.sem.rb, 1)
     s_.activation(T.rb[xs, :], T.da[xs, :], AF.Relu, bias=1.0, scale=-1.0).then_inc(T.sem.rb, 1)
+
+    wait("v", "gb2")
+    v.tensor_scalar(T.b2[0:64, :, :], T.b2i[0:64, :, :], 6, 15, OP.logical_shift_right, OP.bitwise_and).then_inc(
+        T.sem.kb3, 1)
+    v.tensor_scalar(T.b2[xs, :, :], T.b2i[xs, :, :], 63, None, OP.bitwise_and).then_inc(T.sem.kb3, 1)
 
     wait("v", "ldx", 16)
     wait("v", "ldy", 16)
@@ -183,16 +192,14 @@ def rank_program(g, core, T, topo):
     v.tensor_tensor(T.own[xs, 63:128:64], T.own[xs, 63:128:64], T.wl[xs, 2:4], OP.add).then_inc(T.sem.own, 1)
 
     um(3)
-    wait("v", "gb2")
-    v.tensor_scalar(T.b2[0:64, :, :], T.b2i[0:64, :, :], 6, 15, OP.logical_shift_right, OP.bitwise_and).then_inc(
-        T.sem.kb3, 1)
-    v.tensor_scalar(T.b2[xs, :, :], T.b2i[xs, :, :], 63, None, OP.bitwise_and).then_inc(T.sem.kb3, 1)
     wait("v", "ld2", 64)
     v.tensor_scalar(T.wl[xs, 4:6], T.raw2[xs, :, 0, 0], 0.0, 64.0, OP.is_lt, OP.mult).then_inc(T.sem.pr3, 1)
     v.tensor_scalar(T.wl[xs, 6:8], T.raw2[xs, :, 3, 15], 0.0, -64.0, OP.is_gt, OP.mult).then_inc(T.sem.pr3, 1)
     wait("v", "kb3", 2)
     for h in range(2):
         v.tensor_tensor(T.vb[:, :, h, :], T.raw2[:, h, :, :], T.b2[:], OP.add).then_inc(T.sem.pr4, 1)
+    wait("v", "gpc", 3 if edge else 2)
+    v.tensor_scalar(T.p8[:], T.pc[:], 8, None, OP.bitwise_and).then_inc(T.sem.t8, 1)
     wait("v", "pr3", 2)
     wait("v", "pr4", 2)
     v.tensor_tensor(T.vb[xs, 0, :, 0], T.vb[xs, 0, :, 0], T.wl[xs, 4:6], OP.add).then_inc(T.sem.vb, 1)
@@ -297,20 +304,18 @@ def rank_program(g, core, T, topo):
     NPD = {0: 1, 1: 2, 2: 4, 3: 5}
     STEPS = [(1, 1), (2, 2), (4, 4), (8, 8), (16, 1)]
 
-    def image_pads(steps):
+    def image_pads(k):
         wait("s", "ldi", 16)
-        for k in steps:
-            have, cnt = STEPS[k]
-            if k:
-                s_.wait_ge(T.sem.ip, k)
-            if up:
-                f = erow + have
-                dst, src = (f, f + cnt), (f - cnt, f)
-            else:
-                f = erow - have + 1
-                dst, src = (f - cnt, f), (f, f + cnt)
-            s_.activation(T.im[:, dst[0] * W:dst[1] * W], T.im[:, src[0] * W:src[1] * W], AF.Copy).then_inc(
-                T.sem.ip, 1)
+        have, cnt = STEPS[k]
+        if k:
+            s_.wait_ge(T.sem.ip, k)
+        if up:
+            f = erow + have
+            dst, src = (f, f + cnt), (f - cnt, f)
+        else:
+            f = erow - have + 1
+            dst, src = (f - cnt, f), (f, f + cnt)
+        s_.activation(T.im[:, dst[0] * W:dst[1] * W], T.im[:, src[0] * W:src[1] * W], AF.Copy).then_inc(T.sem.ip, 1)
 
     def cast(dst, name, m, take, sem, cnt=1):
         wait("v", "wr" + name, cnt)
@@ -357,13 +362,23 @@ def rank_program(g, core, T, topo):
         z, a, b, nv, c = piece[pn]
         return T.off[:, c + 4 * (x - a):c + 4 * (y - a)]
 
-    def gather(pn):
+    done = set()
+
+    def offsets(pn):
+        if pn in done:
+            return
+        done.add(pn)
         z, a, b, nv, c = piece[pn]
         s, za = zone[z][0:2]
-        lo, hi = a - 2 ** s, b + 2 ** s
         wait("v", "wr" + z)
-        v.tensor_scalar(part(pn, a, b), bank[z][:, 4 * (a - za):4 * (b - za)], float(-W * lo), None, OP.add).then_inc(
-            T.sem["of" + pn], 1)
+        v.tensor_scalar(part(pn, a, b), bank[z][:, 4 * (a - za):4 * (b - za)], float(-W * (a - 2 ** s)), None,
+                        OP.add).then_inc(T.sem["of" + pn], 1)
+
+    def gather(pn):
+        z, a, b, nv, c = piece[pn]
+        s = zone[z][0]
+        lo, hi = a - 2 ** s, b + 2 ** s
+        offsets(pn)
         h = halves(a, b, nv)
         for q in "vs":
             wait(q, "of" + pn)
@@ -442,28 +457,23 @@ def rank_program(g, core, T, topo):
             wait("v", "tc")
             v.tensor_tensor(T.dc[:], T.dti[:], T.tc[:], OP.mult).then_inc(T.sem.dc, 1)
 
-    def list_maker():
-        v.memset(T.bb[:], 0.0).then_inc(T.sem.bb0, 1)
-        v.tensor_scalar(T.e1[:], T.ev[:], 0.0, 64.0, OP.is_equal, OP.mult).then_inc(T.sem.be, 1)
-        v.tensor_scalar(T.e2[:], T.ev[:], 8.0, None, OP.is_equal).then_inc(T.sem.be, 1)
-        wait("v", "be", 2)
-        wait("v", "bb0")
-        v.tensor_tensor(T.bb[:, 15:143:16], T.e1[:], T.e2[:], OP.add).then_inc(T.sem.bb, 1)
-
     wait("t", "own", 2)
     spread("O")
     first_list()
     copies("O")
-    wait("v", "gpc", 3 if edge else 2)
-    v.tensor_scalar(T.p8[:], T.pc[:], 8, None, OP.bitwise_and).then_inc(T.sem.t8, 1)
-    cast(T.fs[:], "0O", 64, -W, "fs", 16)
-    cast(T.fo[:], "0O", 64, 0, "fo", 16)
     shifts()
+    cast(T.fs[:], "0O", 64, -W, "fs", 16)
     if edge:
         copied("v", "O")
         pads(0)
+    cast(T.fo[:], "0O", 64, 0, "fo", 16)
+    v.memset(T.bb[:], 0.0).then_inc(T.sem.bb0, 1)
+    v.tensor_scalar(T.e1[:], T.ev[:], 0.0, 64.0, OP.is_equal, OP.mult).then_inc(T.sem.be, 1)
+    v.tensor_scalar(T.e2[:], T.ev[:], 8.0, None, OP.is_equal).then_inc(T.sem.be, 1)
     gather_own()
-    list_maker()
+    wait("v", "be", 2)
+    wait("v", "bb0")
+    v.tensor_tensor(T.bb[:, 15:143:16], T.e1[:], T.e2[:], OP.add).then_inc(T.sem.bb, 1)
     wait("t", "fs")
     wait("t", "fo")
     copied("t", "O")
@@ -479,13 +489,15 @@ def rank_program(g, core, T, topo):
             last(b)
         elif k == "t":
             turn(b)
+        elif k == "k":
+            offsets(b)
         elif k == "p":
             ready("v", int(b), erow, erow + 1)
             pads(int(b))
         elif k == "i":
-            image_pads((0, 1, 2) if b == "a" else (3, 4))
+            image_pads(int(b))
         else:
-            gather(step)
+            gather(b)
     wait("y", "sty", 32)
     wait("g", "lsd", nls)
     wait("g", "lsl", nll)

from concourse.bass import DstId, RemoteDMATransfer
from concourse.mybir import AluOpType, ActivationFunctionType

W = 64
SCRATCH = {
    "raw": ("sbuf", [128, 128], "int32"),
    "raw2": ("sbuf", [128, 2, 4, 16], "int32"),
    "bi": ("sbuf", [128, 128], "int32"),
    "bj": ("sbuf", [128, 128], "int32"),
    "b2i": ("sbuf", [128, 4, 16], "int32"),
    "b2": ("sbuf", [128, 4, 16], "int32"),
    "wl": ("sbuf", [128, 16], "bfloat16"),
    "own": ("sbuf", [128, 128], "bfloat16"),
    "vb": ("sbuf", [128, 4, 2, 16], "bfloat16"),
    "dd": ("sbuf", [128, 64], "bfloat16"),
    "da": ("sbuf", [128, 64], "bfloat16"),
    "rb": ("sbuf", [128, 64], "bfloat16"),
    "lp": ("sbuf", [128, 128], "bfloat16"),
    "ln": ("sbuf", [128, 128], "bfloat16"),
    "fo": ("sbuf", [128, 64], "uint16"),
    "fs": ("sbuf", [128, 64], "uint16"),
    "fp": ("sbuf", [128, 64], "uint16"),
    "fn": ("sbuf", [128, 64], "uint16"),
    "vi": ("sbuf", [128, 128], "bfloat16"),
    "ua": ("sbuf", [128, 512], "bfloat16"),
    "um": ("sbuf", [128, 1024], "bfloat16"),
    "bb": ("sbuf", [128, 144], "bfloat16"),
    "ev": ("sbuf", [128, 8], "float32"),
    "e1": ("sbuf", [128, 8], "float32"),
    "e2": ("sbuf", [128, 8], "float32"),
    "pc": ("sbuf", [128, 8], "int32"),
    "p8": ("sbuf", [128, 8], "int32"),
    "tc": ("sbuf", [128, 8], "float32"),
    "dti": ("sbuf", [128, 8], "float32"),
    "dc": ("sbuf", [128, 8], "float32"),
    "cp": ("sbuf", [128, 8], "float32"),
    "cn": ("sbuf", [128, 8], "float32"),
    "w0": ("sbuf", [128, 49 * 64], "bfloat16"),
    "w1": ("sbuf", [128, 3072], "bfloat16"),
    "w2": ("sbuf", [128, 3072], "bfloat16"),
    "w3": ("sbuf", [128, 3072], "bfloat16"),
    "im": ("sbuf", [128, 3072], "bfloat16"),
    "ia": ("sbuf", [128, 3072], "bfloat16"),
    "yt": ("sbuf", [128, 1024], "bfloat16"),
    "off": ("sbuf", [128, 640], "uint16"),
}
for _k in range(8):
    SCRATCH["ps%d" % _k] = ("psum", [128, 512], "float32")

ZN = ["0O", "0F", "0L", "1O", "1F", "1L", "1X", "1Y", "2O", "2F", "2L", "3F", "3M", "3L", "4F", "4L"]
SEMAPHORES = ["ldy", "ldx", "ld2", "ldi", "gbi", "gvi", "gb2", "gdd", "gpc", "kb1", "kb2", "kb3", "pr1", "pr2",
              "pr3", "pr4", "own", "vb", "um0", "um1", "um2", "um3", "ua", "us", "da", "rb", "bb0", "be", "bb", "t8",
              "tc", "dc", "arrP", "arrN", "lstP", "lstN", "imgP", "imgN", "iarP", "iarN", "lsd", "lsl", "lsi", "lsa",
              "sty", "ip", "pd0", "pd1", "pd2", "pd3", "m0", "fo", "fs"]
SEMAPHORES += ["u%s%d" % (b, h) for b in "OFL" for h in range(4)]
SEMAPHORES += ["c%s%s" % (b, h) for b in "OFL" for h in "vs"]
SEMAPHORES += ["%s%s" % (k, z) for z in ZN for k in ("wr", "of", "gv", "gs")]

ZONES = {"1O": (7, [("1O", 19, 29, 4)]), "1F": (4, [("1X", 12, 16, 2), ("1F", 16, 19, 2)]),
         "1L": (0, [("1L", 29, 40, 5), ("1Y", 40, 44, 2)]), "2F": (5, [("2F", 16, 24, 4), ("2O", 24, 29, 2)]),
         "2L": (1, [("2L", 29, 40, 5)]), "3F": (6, [("3F", 16, 24, 4)]), "3M": (3, [("3M", 24, 28, 1)]),
         "3L": (2, [("3L", 28, 40, 6)])}
ZEND = {"1O": (7, [("1O", 19, 32, 6)]), "1F": (0, [("1F", 12, 19, 3)]), "2O": (1, [("2L", 24, 32, 4)]),
        "2F": (2, [("2F", 16, 24, 4)]), "3F": (4, [("3F", 16, 24, 4)]), "3L": (3, [("3L", 24, 40, 8)])}
ORDER = ("uF uL t1O cF cL 0F k1O t1F 0L g1O t1L k1F k1X g1F t2F k1L g1X k1Y g1L t2L k2F k2O g2F t3F g1Y k2L g2O "
         "t3M g2L t3L g3F k3M k3L g3M g3L 4L 4F").split()
OEND = ("uF t1O i0 cF p1 i1 0F t1F k1O g1O t2O k1F i2 g1F t2F p2 k2L g2L k2F g2F t3F i3 p3 i4 t3L g3F g3L "
        "4L 4F").split()


def rank_program(g, core, T, topo):
    rank = T.rank_of(core)
    if rank is None:
        return
    OP, AF = AluOpType, ActivationFunctionType
    n = len(T.cores)
    prev = T.cores[rank - 1] if rank > 0 else None
    nxt = T.cores[rank + 1] if rank < n - 1 else None
    same_chip = lambda c: c is not None and topo.chip(c) == topo.chip(core)
    flip = same_chip(nxt)
    edge = prev is None or nxt is None
    sides = {"F": "N" if flip else "P"}
    if not edge:
        sides["L"] = "P" if flip else "N"
    land = {"P": T.lp, "N": T.ln}
    lst = {"P": T.fp, "N": T.fn}
    bias = {"P": T.cp, "N": T.cn}
    blk = {"P": 0, "O": 1, "N": 2}
    vrows = {"0O": 6, "0F": 2, "0L": 6}
    share = {"O": {"s": (0, 1, 2), "v": (3,)}, "F": {"s": (0,), "v": (1,)} if flip else {"s": (2,), "v": (3,)},
             "L": {"s": (0, 2), "v": (1, 3)}}

    def rows(a, b):
        return (48 - b, 48 - a) if flip else (a, b)

    zone, piece = {}, {}
    col = 0
    for name, (bk, parts) in (ZEND if edge else ZONES).items():
        zone[name] = (int(name[0]),) + rows(parts[0][1], parts[-1][2]) + (bk,)
        for pn, a, b, nv in parts:
            piece[pn] = (name,) + rows(a, b) + (nv, col)
            col += 4 * (b - a)
    ps = [T["ps%d" % k] for k in range(8)]
    bank = {z: ps[zone[z][3]] for z in zone}
    bank["0O"] = ps[4]
    ubank = {"O": ps[0:4], "F": [ps[5], ps[6], ps[5], ps[6]], "L": ps[0:4]}
    bse = ps[7]
    erow = 16 if flip else 31
    estep = -1 if flip else 1
    up = estep > 0
    win = [T.w0, T.w1, T.w2, T.w3]

    def wrow(s, a, b, first=0, step=1):
        d = 1 if s == 0 else 0
        return win[s][:, (a + d) * W + first:(b + d) * W:step]

    seen = {"g": set(), "t": set(), "v": set(), "s": set(), "y": set()}
    queue = {"g": g, "t": g.tensor, "v": g.vector, "s": g.scalar, "y": g.sync}

    def wait(q, name, val=1):
        if name in seen[q]:
            return
        seen[q].add(name)
        queue[q].wait_ge(T.sem[name], val)

    g.sync.dma_start(T.raw[0:64, :], T.vy[:]).then_inc(T.sem.ldy, 16)
    g.scalar.dma_start(T.raw[64:128, :], T.vx[:]).then_inc(T.sem.ldx, 16)
    for h in range(2):
        g.sync.dma_start(T.raw2[0:64, h, :, :], T.vy[h::2, :]).then_inc(T.sem.ld2, 16)
        g.scalar.dma_start(T.raw2[64:128, h, :, :], T.vx[h::2, :]).then_inc(T.sem.ld2, 16)
    g.sync.dma_start(T.im[:, 1024:2048], T.img[:]).then_inc(T.sem.ldi, 16)

    xs = slice(64, 128)
    g.iota(T.bi[:], [[64, 2], [1, 64]], 0, 128).then_inc(T.sem.gbi, 1)
    g.iota(T.vi[:], [[-8, 8], [-64, 2], [0, 8]], 0, 1, allow_small_or_imprecise_dtypes=True).then_inc(T.sem.gvi, 1)
    g.iota(T.b2i[:], [[16, 4], [1, 16]], 0, 64).then_inc(T.sem.gb2, 1)
    g.iota(T.dd[:], [[-1, 64]], 0, 1, allow_small_or_imprecise_dtypes=True).then_inc(T.sem.gdd, 1)
    g.iota(T.pc[:], [[0, 8]], 0, 1).then_inc(T.sem.gpc, 1)
    if edge:
        g.iota(T.dti[:], [[estep, 8]], estep, 0, allow_small_or_imprecise_dtypes=True).then_inc(T.sem.gpc, 1)
    g.iota(T.ev[:], [[-16, 8]], 0, 1, allow_small_or_imprecise_dtypes=True).then_inc(T.sem.gpc, 1)

    v, s_, t = g.vector, g.scalar, g.tensor
    if flip:
        v.memset(T.w0[:, 0:W], 0.0).then_inc(T.sem.m0, 1)
        v.memset(T.ia[:, 0:8 * W], 0.0).then_inc(T.sem.m0, 1)
    else:
        v.memset(T.w0[:, 0:9 * W], 0.0).then_inc(T.sem.m0, 2)
    wait("v", "gbi")
    v.tensor_scalar(T.bj[0:64, :], T.bi[0:64, :], 6, 15, OP.logical_shift_right, OP.bitwise_and).then_inc(T.sem.kb1, 1)
    v.tensor_scalar(T.bj[xs, :], T.bi[xs, :], 63, None, OP.bitwise_and).then_inc(T.sem.kb1, 1)
    wait("v", "kb1", 2)
    v.tensor_scalar(bse[0:64, 0:128], T.bj[0:64, :], 16.0, None, OP.add).then_inc(T.sem.kb2, 1)
    v.tensor_scalar(bse[xs, 0:128], T.bj[xs, :], 0.0, None, OP.add).then_inc(T.sem.kb2, 1)

    def um(i):
        v.tensor_scalar(T.um[:, i * 128:(i + 1) * 128], T.vi[:], float(i), None, OP.is_equal).then_inc(
            T.sem["um%d" % i], 1)

    wait("v", "gvi")
    um(0)
    um(1)
    wait("s", "gvi")
    for i in range(4):
        s_.activation(T.ua[:, i * 128:(i + 1) * 128], T.vi[:], AF.Abs, bias=float(-4 - i)).then_inc(T.sem.ua, 1)
    wait("s", "gdd")
    s_.activation(T.da[0:64, :], T.dd[0:64, :], AF.Abs).then_inc(T.sem.da, 1)
    s_.activation(T.da[xs, :], T.dd[xs, :], AF.Abs, bias=-64.0).then_inc(T.sem.da, 1)
    wait("s", "ua", 4)
    for i in range(2):
        s_.activation(T.um[:, 512 + i * 256:768 + i * 256], T.ua[:, i * 256:256 + i * 256], AF.Relu, bias=1.0,
                      scale=-1.0).then_inc(T.sem.us, 1)
    wait("s", "da", 2)
    s_.activation(T.rb[0:64, :], T.da[0:64, :], AF.Relu, bias=64.0, scale=-64.0).then_inc(T.sem.rb, 1)
    s_.activation(T.rb[xs, :], T.da[xs, :], AF.Relu, bias=1.0, scale=-1.0).then_inc(T.sem.rb, 1)

    wait("v", "gb2")
    v.tensor_scalar(T.b2[0:64, :, :], T.b2i[0:64, :, :], 6, 15, OP.logical_shift_right, OP.bitwise_and).then_inc(
        T.sem.kb3, 1)
    v.tensor_scalar(T.b2[xs, :, :], T.b2i[xs, :, :], 63, None, OP.bitwise_and).then_inc(T.sem.kb3, 1)

    wait("v", "ldx", 16)
    wait("v", "ldy", 16)
    wait("v", "kb2", 2)
    v.tensor_tensor(T.own[:], T.raw[:], bse[:, 0:128], OP.add).then_inc(T.sem.pr2, 1)
    v.tensor_scalar(T.wl[xs, 0:2], T.raw[xs, 0:128:64], 0.0, 64.0, OP.is_lt, OP.mult).then_inc(T.sem.pr1, 1)
    v.tensor_scalar(T.wl[xs, 2:4], T.raw[xs, 63:128:64], 0.0, -64.0, OP.is_gt, OP.mult).then_inc(T.sem.pr1, 1)
    um(2)
    wait("v", "pr1", 2)
    wait("v", "pr2")
    v.tensor_tensor(T.own[xs, 0:128:64], T.own[xs, 0:128:64], T.wl[xs, 0:2], OP.add).then_inc(T.sem.own, 1)
    v.tensor_tensor(T.own[xs, 63:128:64], T.own[xs, 63:128:64], T.wl[xs, 2:4], OP.add).then_inc(T.sem.own, 1)

    um(3)
    wait("v", "ld2", 64)
    v.tensor_scalar(T.wl[xs, 4:6], T.raw2[xs, :, 0, 0], 0.0, 64.0, OP.is_lt, OP.mult).then_inc(T.sem.pr3, 1)
    v.tensor_scalar(T.wl[xs, 6:8], T.raw2[xs, :, 3, 15], 0.0, -64.0, OP.is_gt, OP.mult).then_inc(T.sem.pr3, 1)
    wait("v", "kb3", 2)
    for h in range(2):
        v.tensor_tensor(T.vb[:, :, h, :], T.raw2[:, h, :, :], T.b2[:], OP.add).then_inc(T.sem.pr4, 1)
    wait("v", "gpc", 3 if edge else 2)
    v.tensor_scalar(T.p8[:], T.pc[:], 8, None, OP.bitwise_and).then_inc(T.sem.t8, 1)
    wait("v", "pr3", 2)
    wait("v", "pr4", 2)
    v.tensor_tensor(T.vb[xs, 0, :, 0], T.vb[xs, 0, :, 0], T.wl[xs, 4:6], OP.add).then_inc(T.sem.vb, 1)
    v.tensor_tensor(T.vb[xs, 3, :, 15], T.vb[xs, 3, :, 15], T.wl[xs, 6:8], OP.add).then_inc(T.sem.vb, 1)

    dests = [d for d in (prev, nxt) if d is not None]
    offd = [d for d in dests if not same_chip(d)]
    ond = [d for d in dests if same_chip(d)]
    leave = [e for d in offd for e in topo.engines(core, d)]
    half = {d: [e for e in topo.engines(core, d) if not same_chip(d) or e not in leave][-8:] for d in dests}
    every = {d: topo.engines(core, d) for d in ond}

    def send(to, use, src, dst_of, arr_of, local):
        trs, cnt = [], 0
        for d in to:
            rid, pid, _ = topo.addr(d)
            mask = 0
            for e in use[d]:
                mask |= 1 << e
            cnt += len(use[d])
            side = "P" if d == nxt else "N"
            trs.append(RemoteDMATransfer(dst_ids=[DstId(rid=rid, pnc=pid)], dma_engine_mask=mask,
                                         remote_sem=T.sem[arr_of + side], srcs=[src], dsts=[dst_of(side)]))
        g.remote_dma_fused(trs, local_sem=T.sem[local])
        return cnt

    NE = {sd: len(half[c]) for sd, c in (("P", prev), ("N", nxt)) if c is not None}
    NA = len(topo.engines(ond[0], core))
    near = rows(16, 24)
    there = {"P": (8, 16), "N": (32, 40)}
    wait("g", "own", 2)
    nls = send(offd + ond, half, T.own[:], lambda sd: land[sd][:], "arr", "lsd")
    wait("g", "fs")
    nll = send(offd + ond, half, T.fs[:], lambda sd: lst[sd][:], "lst", "lsl")
    wait("g", "ldi", 16)
    nli = 0
    if offd:
        nli += send(offd, half, T.im[:, 1024:2048], lambda sd: T.im[:, blk[sd] * 1024:(blk[sd] + 1) * 1024], "img",
                    "lsi")
    nli += send(ond, half, T.im[:, near[0] * W:near[1] * W], lambda sd: T.im[:, there[sd][0] * W:there[sd][1] * W],
                "img", "lsi")
    wait("g", "gv3F")
    wait("g", "gs3F")
    nla = send(ond, every, T.ia[:, near[0] * W:near[1] * W], lambda sd: T.ia[:, there[sd][0] * W:there[sd][1] * W],
               "iar", "lsa")

    def spread(b):
        src = T.own if b == "O" else land[sides[b]]
        if b != "O":
            wait("t", "arr" + sides[b], NE[sides[b]])
        for i in range(8):
            if i // 2 not in share[b]["s"] + share[b]["v"]:
                continue
            wait("t", "um%d" % i if i < 4 else "us", 1 if i < 4 else 2)
            t.matmul(ubank[b][i // 2][:, (i % 2) * 128:(i % 2 + 1) * 128], T.um[:, i * 128:(i + 1) * 128], src[:],
                     True, True).then_inc(T.sem["u%s%d" % (b, i // 2)], 1)

    def first_list():
        wait("t", "rb", 2)
        wait("t", "pr4", 2)
        wait("t", "vb", 2)
        for a in range(4):
            for b in range(4):
                t.matmul(bank["0O"][32 * a:32 * a + 32, b:64:4], T.vb[:, b, :, :], T.rb[:, 16 * a:16 * a + 16], True,
                         True).then_inc(T.sem["wr0O"], 1)

    def copies(b, qs="sv"):
        base = 16 * blk["O" if b == "O" else sides[b]]
        for q in qs:
            if b != "O":
                wait(q, "dc", 2)
            for k in share[b][q]:
                wait(q, "u%s%d" % (b, k), 2)
                o, i = wrow(0, base + 4 * k, base + 4 * k + 4), ubank[b][k][:, 0:256]
                if q == "v":
                    if b == "O":
                        op = v.tensor_copy(o, i)
                    else:
                        op = v.tensor_scalar(o, i, bias[sides[b]][:, 0:1], None, OP.add)
                elif b == "O":
                    op = s_.activation(o, i, AF.Copy)
                else:
                    op = s_.activation(o, i, AF.Identity, bias=bias[sides[b]][:, 0:1])
                op.then_inc(T.sem["c%s%s" % (b, q)], 1)

    def copied(q, b):
        for e in "vs":
            wait(q, "c%s%s" % (b, e), len(share[b][e]))

    def pads(s):
        wait("v", "dc", 2)
        for d in range(1, min(2 ** s, 4) + 1):
            r = erow + estep * d
            v.tensor_scalar(wrow(s, r, r + 1), wrow(s, erow, erow + 1), T.dc[:, d - 1:d], None, OP.add).then_inc(
                T.sem["pd%d" % s], 1)
        if s == 3:
            v.wait_ge(T.sem.pd3, 4)
            a = erow + 1 if up else erow - 4
            v.tensor_scalar(wrow(s, a + 4 * estep, a + 4 * estep + 4), wrow(s, a, a + 4), T.dc[:, 3:4], None,
                            OP.add).then_inc(T.sem.pd3, 1)

    NPD = {0: 1, 1: 2, 2: 4, 3: 5}
    STEPS = [(1, 1), (2, 2), (4, 4), (8, 8), (16, 1)]

    def image_pads(k):
        wait("s", "ldi", 16)
        have, cnt = STEPS[k]
        if k:
            s_.wait_ge(T.sem.ip, k)
        if up:
            f = erow + have
            dst, src = (f, f + cnt), (f - cnt, f)
        else:
            f = erow - have + 1
            dst, src = (f - cnt, f), (f, f + cnt)
        s_.activation(T.im[:, dst[0] * W:dst[1] * W], T.im[:, src[0] * W:src[1] * W], AF.Copy).then_inc(T.sem.ip, 1)

    def cast(dst, name, m, take, sem, cnt=1):
        wait("v", "wr" + name, cnt)
        v.tensor_scalar(dst, bank[name][:, 0:m], float(-take), None, OP.add).then_inc(T.sem[sem], 1)

    def pick(q, out, w, li, sem):
        if q == "v":
            v.tensor_copy(out, w.indirect(li)).then_inc(T.sem["gv" + sem], 1)
        else:
            s_.activation(out, w.indirect(li), AF.Copy).then_inc(T.sem["gs" + sem], 1)

    def halves(a, b, nv):
        return {"v": (b - nv, b), "s": (a, b - nv)} if flip else {"v": (a, a + nv), "s": (a + nv, b)}

    def both(name, nv=1):
        return [("gv" + name, nv), ("gs" + name, 1)]

    made = {1: [(rows(17, 32 if edge else 31), both("0O")), (rows(10, 17), both("0F", 2))], 2: [], 3: [], 4: []}
    if edge:
        for s in (1, 2, 3):
            made[s].append((rows(32, 32 + 2 ** s), [("pd%d" % s, NPD[s])]))
    else:
        made[1].append((rows(31, 46), both("0L", 2)))
    for pn, (z, a, b, nv, c) in piece.items():
        made[zone[z][0] + 1].append(((a, b), both(pn)))
    made[4].append((rows(8, 16), [("iar" + sides["F"], NA)]))

    def ready(q, s, a, b):
        for (x, y), sems in made[s]:
            if x < b and a < y:
                for nm, val in sems:
                    wait(q, nm, val)

    def turn(name):
        s, a, b, bk = zone[name]
        ready("t", s, a, b)
        wait("t", "bb")
        m = 4 * (b - a)
        for q in range(16):
            mm = t.matmul(bank[name][:, 0:m], T.bb[:, 15 - q:143 - q], wrow(s, a, b, q, 16), q == 0, q == 15)
        mm.then_inc(T.sem["wr" + name], 1)

    def part(pn, x, y):
        z, a, b, nv, c = piece[pn]
        return T.off[:, c + 4 * (x - a):c + 4 * (y - a)]

    done = set()

    def offsets(pn):
        if pn in done:
            return
        done.add(pn)
        z, a, b, nv, c = piece[pn]
        s, za = zone[z][0:2]
        wait("v", "wr" + z)
        v.tensor_scalar(part(pn, a, b), bank[z][:, 4 * (a - za):4 * (b - za)], float(-W * (a - 2 ** s)), None,
                        OP.add).then_inc(T.sem["of" + pn], 1)

    def gather(pn):
        z, a, b, nv, c = piece[pn]
        s = zone[z][0]
        lo, hi = a - 2 ** s, b + 2 ** s
        offsets(pn)
        h = halves(a, b, nv)
        for q in "vs":
            wait(q, "of" + pn)
            x, y = h[q]
            if s < 3:
                ready(q, s, lo, hi)
                pick(q, wrow(s + 1, x, y), wrow(s, lo, hi), part(pn, x, y), pn)
            else:
                wait(q, "ldi", 16)
                for sd, out in (("P", lo < 16), ("N", hi > 32)):
                    if out and sd in NE:
                        wait(q, "img" + sd, NE[sd])
                    elif out:
                        wait(q, "ip", 5)
                pick(q, T.ia[:, x * W:y * W], T.im[:, lo * W:hi * W], part(pn, x, y), pn)

    def gather_own():
        if edge:
            a, b = rows(17, 32)
            li, wl, wh = ("fs", 15, 32) if prev is None else ("fo", 16, 33)
        else:
            a, b, li, wl, wh = 17, 31, "fo", 16, 32
        h = halves(a, b, vrows["0O"])
        for q in "vs":
            wait(q, li)
            if edge:
                wait(q, "pd0")
            copied(q, "O")
            x, y = h[q]
            pick(q, wrow(1, x, y), wrow(0, wl, wh), T[li][:, 4 * (x - 16):4 * (y - 16)], "0O")

    def gather_side(b):
        sd = sides[b]
        cnt = 6 if b == "F" else 14
        if sd == "P":
            a, e, r0, wl, wh = 16 - cnt, 16, 0, -1, 17
            one, li, ol, oh = 16, "fs", 15, 18
        else:
            a, e, r0, wl, wh = 32, 32 + cnt, 32, 31, 33 + cnt
            one, li, ol, oh = 31, "fo", 16, 33
        nv = vrows["0" + b]
        for q, x, y in (("v", a, a + nv), ("s", a + nv, e)):
            copied(q, "O")
            copied(q, b)
            if q == "v":
                wait(q, li)
                pick(q, wrow(1, one, one + 1), wrow(0, ol, oh), T[li][:, 4 * (one - 16):4 * (one - 15)], "0" + b)
            if sd == "P":
                wait(q, "m0", 2)
            wait(q, "lst" + sd, NE[sd])
            pick(q, wrow(1, x, y), wrow(0, wl, wh), lst[sd][:, 4 * (x - r0):4 * (y - r0)], "0" + b)

    def last(b):
        a, e = rows(16, 24) if b == "F" else rows(24, 32)
        h = halves(a, e, 4)
        for q in "vs":
            x, y = h[q]
            pn = [k for k in piece if k[0] == "3" and piece[k][1] <= x and y <= piece[k][2]][0]
            lo = piece[pn][1] - 8
            ready(q, 4, lo, y + 8)
            wait(q, "m0", 2)
            pick(q, T.yt[:, (x - 16) * W:(y - 16) * W], T.ia[:, lo * W:(y + 8) * W], part(pn, x, y), "4" + b)
        for nm, val in both("4" + b):
            wait("y", nm, val)
        cols = slice((a - 16) * W, (e - 16) * W)
        g.sync.dma_start(T.y[:, cols], T.yt[:, cols]).then_inc(T.sem.sty, 16)

    def shifts():
        wait("v", "t8")
        if edge:
            v.tensor_scalar(T.tc[:], T.p8[:], 0.0, None, OP.is_equal).then_inc(T.sem.tc, 1)
        for sd, val in (("P", -16.0), ("N", 16.0)):
            if sd in sides.values():
                v.tensor_scalar(bias[sd][:], T.p8[:], 0.0, val, OP.is_equal, OP.mult).then_inc(T.sem.dc, 1)
        if edge:
            wait("v", "tc")
            v.tensor_tensor(T.dc[:], T.dti[:], T.tc[:], OP.mult).then_inc(T.sem.dc, 1)

    wait("t", "own", 2)
    spread("O")
    first_list()
    copies("O")
    shifts()
    cast(T.fs[:], "0O", 64, -W, "fs", 16)
    if edge:
        copied("v", "O")
        pads(0)
    cast(T.fo[:], "0O", 64, 0, "fo", 16)
    v.memset(T.bb[:], 0.0).then_inc(T.sem.bb0, 1)
    v.tensor_scalar(T.e1[:], T.ev[:], 0.0, 64.0, OP.is_equal, OP.mult).then_inc(T.sem.be, 1)
    v.tensor_scalar(T.e2[:], T.ev[:], 8.0, None, OP.is_equal).then_inc(T.sem.be, 1)
    gather_own()
    wait("v", "be", 2)
    wait("v", "bb0")
    v.tensor_tensor(T.bb[:, 15:143:16], T.e1[:], T.e2[:], OP.add).then_inc(T.sem.bb, 1)
    wait("t", "fs")
    wait("t", "fo")
    copied("t", "O")
    for step in (OEND if edge else ORDER):
        k, b = step[0], step[1:]
        if k == "u":
            spread(b)
        elif k == "c":
            copies(b)
        elif k == "0":
            gather_side(b)
        elif k == "4":
            last(b)
        elif k == "t":
            turn(b)
        elif k == "k":
            offsets(b)
        elif k == "p":
            ready("v", int(b), erow, erow + 1)
            pads(int(b))
        elif k == "i":
            image_pads(int(b))
        else:
            gather(b)
    wait("y", "sty", 32)
    wait("g", "lsd", nls)
    wait("g", "lsl", nll)
    wait("g", "lsi", nli)
    wait("g", "lsa", nla)
